import numpy as np, ml_dtypes
CORES = [52,68,84,180,196,212,308,324,340]
N = 9
R, T = 4096, 1024
CAPP = 256
def entries(a): return a.T.reshape(-1)
def pack(v, P): return np.ascontiguousarray(np.asarray(v, np.int32).reshape(-1, P).T)
def lists(rng, how):
    I = rng.integers(0, N * R, (N, T))
    O = np.stack([rng.permutation(np.repeat(np.arange(N), CAPP))[:T] for r in range(N)])
    if how == "full": O = np.stack([rng.permutation(np.repeat(rng.permutation(N)[:T // CAPP], CAPP)) for r in range(N)])
    I = R * O + rng.integers(0, R, (N, T))
    if how == "alike": I = R * O + rng.integers(0, R, (N, 1))
    if how == "edge": I = R * O + np.where(rng.random((N, T)) < 0.5, 0, R - 1)
    if how == "sorted": I = np.sort(I, axis=1)
    return {"idx": np.stack([pack(I[r], 16) for r in range(N)])}
def setup_inputs(rng):
    return dict({"tab": rng.standard_normal((N, 128, R), dtype=np.float32).astype(ml_dtypes.bfloat16)}, **lists(rng, "uniform"))
def setup_inputs_alike(rng):
    d = setup_inputs(rng); d.update(lists(rng, "alike"))
    for k in ("tab",): d[k] = (d[k].astype(np.float32) * 1048576.0).astype(d[k].dtype)
    return d
def setup_inputs_edge(rng):
    d = setup_inputs(rng); d.update(lists(rng, "edge"))
    for k in ("tab",): d[k] = (d[k].astype(np.float32) * (1 / 1024.0)).astype(d[k].dtype)
    return d
def setup_inputs_full(rng):
    d = setup_inputs(rng); d.update(lists(rng, "full"))
    return d
def setup_inputs_sorted(rng):
    d = setup_inputs(rng); d.update(lists(rng, "sorted"))
    return d
def check_inputs(x):
    bad = []
    if x["idx"].min() < 0 or x["idx"].max() >= N * R: bad.append("idx out of range")
    if max(int(np.bincount(entries(a) // R, minlength=N).max()) for a in x["idx"]) > CAPP: bad.append("more than CAPP entries of a list point into one rank's part")
    return bad
def reference(tab, idx):
    A = np.concatenate(list(tab), axis=1)
    return {"y": np.stack([A[:, entries(idx[r])] for r in range(N)])}

@@ -1,0 +1,269 @@
+from concourse.bass import DstId, RemoteDMATransfer
+from concourse.mybir import AluOpType, ActivationFunctionType
+
+N, R, L, CAP = 9, 4096, 1024, 256
+NE = 80
+
+SCRATCH = {
+    "tabs": ("sbuf", [128, R], "bfloat16"),
+    "land": ("sbuf", [128, N * CAP], "bfloat16"),
+    "stage": ("sbuf", [128, N * CAP], "bfloat16"),
+    "ybuf": ("sbuf", [128, L], "bfloat16"),
+    "ent": ("sbuf", [128, 8], "int32"),
+    "own_i": ("sbuf", [128, 8], "int32"),
+    "loc_i": ("sbuf", [128, 8], "int32"),
+    "own_f": ("sbuf", [128, 8], "float32"),
+    "locm": ("sbuf", [128, 8], "float32"),
+    "oval": ("sbuf", [128, 72], "float32"),
+    "mk": ("sbuf", [128, 72], "float32"),
+    "c256": ("sbuf", [128, 72], "bfloat16"),
+    "hpad": ("sbuf", [128, 136], "bfloat16"),
+    "onesb": ("sbuf", [128, 1024], "bfloat16"),
+    "tri": ("sbuf", [128, 128], "bfloat16"),
+    "sel": ("sbuf", [128, 1024], "bfloat16"),
+    "i16": ("sbuf", [128, 128], "bfloat16"),
+    "i144": ("sbuf", [128, 144], "bfloat16"),
+    "zz": ("sbuf", [128, 72], "float32"),
+    "sc": ("sbuf", [128, 72], "float32"),
+    "slot_i": ("sbuf", [128, 8], "int32"),
+    "hl_i": ("sbuf", [128, 24], "int32"),
+    "hl_f": ("sbuf", [128, 16], "float32"),
+    "hlb": ("sbuf", [128, 16], "bfloat16"),
+    "lt": ("sbuf", [128, 1024], "float16"),
+    "rh": ("sbuf", [128, 1152], "float16"),
+    "offs": ("sbuf", [128, 16 * N], "uint16"),
+    "rq": ("sbuf", [128, 16 * N], "uint16"),
+    "fin": ("sbuf", [128, 64], "uint16"),
+    "pp": ("psum", [128, 512], "float32"),
+    "pr": ("psum", [128, 512], "float32"),
+    "pf": ("psum", [128, 512], "float32"),
+}
+SEMAPHORES = (["e%d" % i for i in range(NE)] + ["rq%d" % i for i in range(N)]
+              + ["resp", "sent", "rreq", "rresp", "idxl", "tabl", "st0", "st1"])
+
+_CACHE = {}
+
+
+def _bits(m):
+    return [i for i in range(16) if (m >> i) & 1]
+
+
+def _plan(T, topo):
+    if "p" in _CACHE:
+        return _CACHE["p"]
+    cores = list(T.cores)
+    n = len(cores)
+    world = range(4 * topo.CORES_PER_HOST)
+    rank_hosts = set(topo.host(c) for c in cores)
+    relay = {}
+    for r in range(n):
+        for o in range(n):
+            cr, co = cores[r], cores[o]
+            if r == o or topo.may_write(cr, co):
+                continue
+            far = near = None
+            chipc = []
+            for h in range(4):
+                if h in rank_hosts:
+                    continue
+                far, near = (cr, co) if topo.rack(topo.host(cr)) != topo.rack(h) else (co, cr)
+                chipc = [x for x in world if topo.host(x) == h and topo.chip(x) == topo.chip(far)]
+                if all(topo.may_write(cr, x) and topo.may_write(x, co) and topo.may_write(co, x)
+                       and topo.may_write(x, cr) for x in chipc):
+                    break
+            other = [x for x in chipc if topo.die(x) != topo.die(far)]
+            same = [x for x in chipc if topo.die(x) == topo.die(far)]
+            k = [c for c in cores if topo.host(c) == topo.host(near)].index(near)
+            if far == cr:
+                relay[(r, o)] = [same[0], same[2], other[3]][k]
+            else:
+                relay[(r, o)] = other[k]
+
+    def kind(a, b):
+        if (a, b) in relay:
+            return 0
+        return 1 if topo.rack(topo.host(cores[a])) != topo.rack(topo.host(cores[b])) else 2
+    req_order = [sorted([o for o in range(n) if o != r], key=lambda o: (kind(r, o), (o - r) % n)) for r in range(n)]
+    resp_order = [sorted([r for r in range(n) if r != o],
+                         key=lambda r: (-kind(r, o), req_order[r].index(o), (r - o) % n)) for o in range(n)]
+    p = {"cores": cores, "relay": relay, "req": req_order, "resp": resp_order,
+         "by_relay": dict((v, k) for k, v in relay.items())}
+    _CACHE["p"] = p
+    return p
+
+
+def _relay_program(g, core, T, topo, p, r, o):
+    cr, co = p["cores"][r], p["cores"][o]
+    m = topo.mask(core, co)
+    rid, pid = topo.addr(co, core)
+    g.wait_ge(T.sem.rreq, 2)
+    g.remote_dma(T.rq[:, 16 * r:16 * r + 16], T.rq[:, 0:16], T.sem["rq%d" % r], T.sem.sent, pid, rid, m)
+    m2 = topo.mask(core, cr)
+    rid, pid = topo.addr(cr, core)
+    g.wait_ge(T.sem.rresp, 2)
+    g.remote_dma(T.land[:, CAP * o:CAP * o + CAP], T.land[:, 0:CAP], T.sem.resp, T.sem.sent, pid, rid, m2)
+    g.wait_ge(T.sem.sent, len(_bits(m)) + len(_bits(m2)))
+
+
+def rank_program(g, core, T, topo):
+    p = _plan(T, topo)
+    me = T.rank_of(core)
+    if me is None:
+        if core in p["by_relay"]:
+            r, o = p["by_relay"][core]
+            _relay_program(g, core, T, topo, p, r, o)
+        return
+    cores, relay = p["cores"], p["relay"]
+    V, PE, S, SY = g.vector, g.tensor, g.scalar, g.sync
+    A = AluOpType
+    cnt = [0]
+
+    def ev():
+        cnt[0] += 1
+        return T.sem["e%d" % (cnt[0] - 1)]
+
+    SY.dma_start(T.ent[:, :], T.idx[:, :]).then_inc(T.sem.idxl, 16)
+    SY.dma_start(T.tabs[:, :], T.tab[:, :]).then_inc(T.sem.tabl, 16)
+
+    e_ones, e_hz, e_oval, e_tri, e_i16, e_i144, e_sel, e_mk, e_c = [ev() for _ in range(9)]
+    V.memset(T.onesb[:, :], 1.0).then_inc(e_ones, 1)
+    V.memset(T.hpad[:, 0:64], 0.0).then_inc(e_hz, 1)
+    g.iota(T.oval[:, :], [[0, 8], [1, 9]], 0, 0, allow_small_or_imprecise_dtypes=True).then_inc(e_oval, 1)
+    g.wait_ge(e_ones, 1)
+    g.affine_select(T.tri[:, :], T.onesb[:, 0:128], [[1, 128]], A.is_gt, 0.0, 0, -1).then_inc(e_tri, 1)
+    g.iota(T.i16[:, :], [[0, 8], [1, 16]], 0, 0, allow_small_or_imprecise_dtypes=True).then_inc(e_i16, 1)
+    g.iota(T.i144[:, :], [[1, 144]], 0, 0, allow_small_or_imprecise_dtypes=True).then_inc(e_i144, 1)
+    g.affine_select(T.sel[:, :], T.onesb[:, :], [[-1, 8], [0, 8], [-8, 16]], A.is_equal, 0.0, 0, 1).then_inc(e_sel, 1)
+    V.wait_ge(e_oval, 1)
+    V.tensor_scalar(T.mk[:, :], T.oval[:, :], 1.0, None, A.min).then_inc(e_mk, 1)
+    V.tensor_scalar(T.c256[:, :], T.oval[:, :], 256.0, None, A.mult).then_inc(e_c, 1)
+
+    e1, e2, e3, e4, eH, eP, eZ, eS, e5, e6, e7, e8, eR, eO, eF, eFin, eself, ey0, ey1 = [ev() for _ in range(19)]
+    V.wait_ge(T.sem.idxl, 16)
+    V.tensor_scalar(T.own_i[:, :], T.ent[:, :], 12, None, A.logical_shift_right).then_inc(e1, 1)
+    V.tensor_scalar(T.loc_i[:, :], T.ent[:, :], R - 1, None, A.bitwise_and).then_inc(e2, 1)
+    V.wait_ge(e1, 1)
+    V.tensor_copy(T.own_f[:, :], T.own_i[:, :]).then_inc(e3, 1)
+    V.wait_ge(e3, 1)
+    for b in range(8):
+        V.tensor_scalar(T.hpad[:, 64 + 9 * b:73 + 9 * b], T.oval[:, 0:9], T.own_f[:, b:b + 1], None,
+                        A.is_equal).then_inc(eH, 1)
+    V.wait_ge(e2, 1)
+    V.tensor_scalar(T.locm[:, :], T.loc_i[:, :], -2048.0, None, A.add).then_inc(e4, 1)
+
+    for s, v in ((eH, 8), (e_hz, 1), (e_tri, 1), (e_ones, 1), (e_c, 1)):
+        PE.wait_ge(s, v)
+    PE.matmul(T.pp[:, 0:72], T.tri[:, :], T.hpad[:, 64:136], True, False).then_inc(eP, 1)
+    for k in range(1, 8):
+        PE.matmul(T.pp[:, 0:72], T.onesb[:, 0:128], T.hpad[:, 64 - 9 * k:136 - 9 * k], False, False).then_inc(eP, 1)
+    PE.matmul(T.pp[:, 0:72], T.onesb[0:1, 0:128], T.c256[0:1, :], False, True).then_inc(eP, 1)
+
+    V.wait_ge(eP, 9)
+    V.wait_ge(eH, 8)
+    V.tensor_tensor(T.zz[:, :], T.pp[:, 0:72], T.hpad[:, 64:136], A.mult).then_inc(eZ, 1)
+    V.wait_ge(eZ, 1)
+    V.wait_ge(e_mk, 1)
+    V.tensor_tensor_scan(T.sc[:, :], T.mk[:, :], T.zz[:, :], 0.0, A.mult, A.add).then_inc(eS, 1)
+    V.wait_ge(eS, 1)
+    V.tensor_copy(T.slot_i[:, :], T.sc[:, 8:72:9]).then_inc(e5, 1)
+    V.wait_ge(e5, 1)
+    V.tensor_scalar(T.hl_i[:, 0:8], T.slot_i[:, :], 4, None, A.logical_shift_right).then_inc(e6, 1)
+    V.tensor_scalar(T.hl_i[:, 8:16], T.slot_i[:, :], 15, None, A.bitwise_and).then_inc(e6, 1)
+    V.tensor_scalar(T.hl_i[:, 16:24], T.slot_i[:, :], 4080, None, A.bitwise_and).then_inc(e6, 1)
+    V.wait_ge(e6, 3)
+    V.tensor_copy(T.hl_f[:, :], T.hl_i[:, 0:16]).then_inc(e7, 1)
+    V.wait_ge(e7, 1)
+    V.wait_ge(e4, 1)
+    V.wait_ge(e_i16, 1)
+    V.wait_ge(e_i144, 1)
+
+    for b in range(8):
+        eb = ev()
+        V.tensor_scalar(T.lt[:, 128 * b:128 * b + 128], T.i16[:, :], T.hl_f[:, 8 + b:9 + b], None,
+                        A.is_equal).then_inc(eb, 1)
+        V.tensor_scalar(T.rh[:, 144 * b:144 * b + 144], T.i144[:, :], T.hl_f[:, b:b + 1], T.locm[:, b:b + 1],
+                        A.is_equal, A.mult).then_inc(eb, 1)
+        PE.wait_ge(eb, 2)
+        PE.matmul(T.pr[:, 0:144], T.lt[:, 128 * b:128 * b + 128], T.rh[:, 144 * b:144 * b + 144],
+                  b == 0, b == 7).then_inc(eR, 1)
+    V.wait_ge(eR, 8)
+    V.tensor_scalar(T.offs[:, :], T.pr[:, 0:144], 2048.0, None, A.add).then_inc(eO, 1)
+
+    def fused(items):
+        eng = [i for i in range(16) if all((topo.mask(core, d) >> i) & 1 for d, _, _, _ in items)]
+        per = len(eng) // len(items)
+        tr = []
+        for k, (d, src, dst, sem) in enumerate(items):
+            rid, pid = topo.addr(d, core)
+            tr.append(RemoteDMATransfer(dst_ids=[DstId(rid=rid, pnc=pid)],
+                                        dma_engine_mask=sum(1 << e for e in eng[per * k:per * k + per]),
+                                        remote_sem=sem, src=src, dst=dst))
+        g.remote_dma_fused(tr, local_sem=T.sem.sent)
+        return per * len(items)
+
+    sent = 0
+    g.wait_ge(eO, 1)
+    for part in (p["req"][me][0:4], p["req"][me][4:8]):
+        items = []
+        for o in part:
+            src = T.offs[:, 16 * o:16 * o + 16]
+            if (me, o) in relay:
+                items.append((relay[(me, o)], src, T.rq[:, 0:16], T.sem.rreq))
+            else:
+                items.append((cores[o], src, T.rq[:, 16 * me:16 * me + 16], T.sem["rq%d" % me]))
+        sent += fused(items)
+
+    V.tensor_copy(T.hlb[:, :], T.hl_i[:, 8:24]).then_inc(e8, 1)
+    PE.wait_ge(e8, 1)
+    PE.wait_ge(e_sel, 1)
+    for h in range(8):
+        PE.matmul(T.pf[:, 8 * h:8 * h + 8], T.sel[:, 128 * h:128 * h + 128], T.hlb[:, 0:8], True, False).then_inc(eF, 1)
+        PE.matmul(T.pf[:, 8 * h:8 * h + 8], T.sel[:, 128 * h:128 * h + 128], T.hlb[:, 8:16], False, True).then_inc(eF, 1)
+    V.wait_ge(eF, 16)
+    V.tensor_copy(T.fin[:, :], T.pf[:, 0:64]).then_inc(eFin, 1)
+
+    S.wait_ge(eO, 1)
+    S.wait_ge(T.sem.tabl, 16)
+    V.wait_ge(T.sem.tabl, 16)
+    S.activation(T.land[:, CAP * me:CAP * me + CAP], T.tabs[:, 0:R].indirect(T.offs[:, 16 * me:16 * me + 16]),
+                 ActivationFunctionType.Copy).then_inc(eself, 1)
+    gs = {}
+    for k, r in enumerate(p["resp"][me]):
+        gs[r] = ev()
+        arr = len(_bits(topo.mask(relay[(r, me)], core))) if (r, me) in relay else 2
+        win = T.tabs[:, 0:R].indirect(T.rq[:, 16 * r:16 * r + 16])
+        out = T.stage[:, CAP * r:CAP * r + CAP]
+        if k % 2 == 0:
+            S.wait_ge(T.sem["rq%d" % r], arr)
+            S.activation(out, win, ActivationFunctionType.Copy).then_inc(gs[r], 1)
+        else:
+            V.wait_ge(T.sem["rq%d" % r], arr)
+            V.tensor_copy(out, win).then_inc(gs[r], 1)
+    for part in (p["resp"][me][0:4], p["resp"][me][4:8]):
+        items = []
+        for r in part:
+            g.wait_ge(gs[r], 1)
+            src = T.stage[:, CAP * r:CAP * r + CAP]
+            if (r, me) in relay:
+                items.append((relay[(r, me)], src, T.land[:, 0:CAP], T.sem.rresp))
+            else:
+                items.append((cores[r], src, T.land[:, CAP * me:CAP * me + CAP], T.sem.resp))
+        sent += fused(items)
+
+    total = sum(len(_bits(topo.mask(relay[(me, o)], core))) if (me, o) in relay else 2 for o in range(N) if o != me)
+    V.wait_ge(eFin, 1)
+    V.wait_ge(eself, 1)
+    V.wait_ge(T.sem.resp, total)
+    V.tensor_copy(T.ybuf[:, 0:512], T.land[:, 0:N * CAP].indirect(T.fin[:, 0:32])).then_inc(ey0, 1)
+    S.wait_ge(eFin, 1)
+    S.wait_ge(eself, 1)
+    S.wait_ge(T.sem.resp, total)
+    S.activation(T.ybuf[:, 512:1024], T.land[:, 0:N * CAP].indirect(T.fin[:, 32:64]),
+                 ActivationFunctionType.Copy).then_inc(ey1, 1)
+    SY.wait_ge(ey0, 1)
+    SY.dma_start(T.y[:, 0:512], T.ybuf[:, 0:512]).then_inc(T.sem.st0, 16)
+    S.wait_ge(ey1, 1)
+    S.dma_start(T.y[:, 512:1024], T.ybuf[:, 512:1024]).then_inc(T.sem.st1, 16)
+    SY.wait_ge(T.sem.st0, 16)
+    S.wait_ge(T.sem.st1, 16)
+    g.wait_ge(T.sem.sent, sent)

@@ -79,14 +79,47 @@ def _plan(T, topo):
             else:
                 relay[(r, o)] = other[k]
 
-    def kind(a, b):
-        if (a, b) in relay:
-            return 0
-        return 1 if topo.rack(topo.host(cores[a])) != topo.rack(topo.host(cores[b])) else 2
-    req_order = [sorted([o for o in range(n) if o != r], key=lambda o: (kind(r, o), (o - r) % n)) for r in range(n)]
-    resp_order = [sorted([r for r in range(n) if r != o],
-                         key=lambda r: (-kind(r, o), req_order[r].index(o), (r - o) % n)) for o in range(n)]
-    p = {"cores": cores, "relay": relay, "req": req_order, "resp": resp_order,
+    def hidx(a):
+        return [c for c in cores if topo.host(c) == topo.host(cores[a])].index(cores[a])
+
+    def outer(a):
+        return any((a, x) in relay for x in range(n))
+
+    reqc = []
+    for r in range(n):
+        k = hidx(r)
+        rel = sorted([o for o in range(n) if (r, o) in relay], key=lambda o: (hidx(o) - k) % n)
+        rest = [o for o in range(n) if o != r and (r, o) not in relay]
+        if rel:
+            mids = [o for o in rest if not outer(o)]
+            d0 = mids[k % len(mids)]
+            reqc.append([[o] for o in rel] + [[d0], [o for o in rest if o != d0]])
+        else:
+            early = [o for o in rest if topo.host(cores[o]) == topo.host(cores[r]) or hidx(o) == k]
+            reqc.append([early, [o for o in rest if o not in early]])
+
+    def per(src, dests):
+        return min(len(_bits(topo.mask(src, d))) for d in dests) // len(dests)
+
+    reqe, when = {}, {}
+    for r in range(n):
+        t = 0
+        for call in reqc[r]:
+            t += len(call)
+            e = per(cores[r], [relay.get((r, o), cores[o]) for o in call])
+            for o in call:
+                reqe[(r, o)], when[(r, o)] = e, t
+    respc, respe = [], {}
+    for o in range(n):
+        late = sorted([r for r in range(n) if (r, o) in relay], key=lambda r: when[(r, o)])
+        d = sorted([r for r in range(n) if r != o and (r, o) not in relay], key=lambda r: (when[(r, o)], (r - o) % n))
+        calls = [[r] for r in late] + ([[d[0]], d[1:]] if late else [d[0:len(d) // 2], d[len(d) // 2:]])
+        respc.append(calls)
+        for call in calls:
+            e = per(cores[o], [relay.get((r, o), cores[r]) for r in call])
+            for r in call:
+                respe[(r, o)] = e
+    p = {"cores": cores, "relay": relay, "reqc": reqc, "respc": respc, "reqe": reqe, "respe": respe,
          "by_relay": dict((v, k) for k, v in relay.items())}
     _CACHE["p"] = p
     return p
@@ -96,11 +129,11 @@ def _relay_program(g, core, T, topo, p, r, o):
     cr, co = p["cores"][r], p["cores"][o]
     m = topo.mask(core, co)
     rid, pid = topo.addr(co, core)
-    g.wait_ge(T.sem.rreq, 2)
+    g.wait_ge(T.sem.rreq, p["reqe"][(r, o)])
     g.remote_dma(T.rq[:, 16 * r:16 * r + 16], T.rq[:, 0:16], T.sem["rq%d" % r], T.sem.sent, pid, rid, m)
     m2 = topo.mask(core, cr)
     rid, pid = topo.addr(cr, core)
-    g.wait_ge(T.sem.rresp, 2)
+    g.wait_ge(T.sem.rresp, p["respe"][(r, o)])
     g.remote_dma(T.land[:, CAP * o:CAP * o + CAP], T.land[:, 0:CAP], T.sem.resp, T.sem.sent, pid, rid, m2)
     g.wait_ge(T.sem.sent, len(_bits(m)) + len(_bits(m2)))
 
@@ -141,13 +174,13 @@ def rank_program(g, core, T, topo):
     e1, e2, e3, e4, eH, eP, eZ, eS, e5, e6, e7, e8, eR, eO, eF, eFin, eself, ey0, ey1 = [ev() for _ in range(19)]
     V.wait_ge(T.sem.idxl, 16)
     V.tensor_scalar(T.own_i[:, :], T.ent[:, :], 12, None, A.logical_shift_right).then_inc(e1, 1)
-    V.tensor_scalar(T.loc_i[:, :], T.ent[:, :], R - 1, None, A.bitwise_and).then_inc(e2, 1)
     V.wait_ge(e1, 1)
     V.tensor_copy(T.own_f[:, :], T.own_i[:, :]).then_inc(e3, 1)
     V.wait_ge(e3, 1)
     for b in range(8):
         V.tensor_scalar(T.hpad[:, 64 + 9 * b:73 + 9 * b], T.oval[:, 0:9], T.own_f[:, b:b + 1], None,
                         A.is_equal).then_inc(eH, 1)
+    V.tensor_scalar(T.loc_i[:, :], T.ent[:, :], R - 1, None, A.bitwise_and).then_inc(e2, 1)
     V.wait_ge(e2, 1)
     V.tensor_scalar(T.locm[:, :], T.loc_i[:, :], -2048.0, None, A.add).then_inc(e4, 1)
 
@@ -203,7 +236,7 @@ def rank_program(g, core, T, topo):
 
     sent = 0
     g.wait_ge(eO, 1)
-    for part in (p["req"][me][0:4], p["req"][me][4:8]):
+    for part in p["reqc"][me]:
         items = []
         for o in part:
             src = T.offs[:, 16 * o:16 * o + 16]
@@ -228,18 +261,20 @@ def rank_program(g, core, T, topo):
     S.activation(T.land[:, CAP * me:CAP * me + CAP], T.tabs[:, 0:R].indirect(T.offs[:, 16 * me:16 * me + 16]),
                  ActivationFunctionType.Copy).then_inc(eself, 1)
     gs = {}
-    for k, r in enumerate(p["resp"][me]):
+    order = [r for call in p["respc"][me] for r in call]
+    has_late = any((r, me) in relay for r in order)
+    for k, r in enumerate(order):
         gs[r] = ev()
-        arr = len(_bits(topo.mask(relay[(r, me)], core))) if (r, me) in relay else 2
+        arr = len(_bits(topo.mask(relay[(r, me)], core))) if (r, me) in relay else p["reqe"][(r, me)]
         win = T.tabs[:, 0:R].indirect(T.rq[:, 16 * r:16 * r + 16])
         out = T.stage[:, CAP * r:CAP * r + CAP]
-        if k % 2 == 0:
+        if ((r, me) in relay) if has_late else (k % 2 == 0):
             S.wait_ge(T.sem["rq%d" % r], arr)
             S.activation(out, win, ActivationFunctionType.Copy).then_inc(gs[r], 1)
         else:
             V.wait_ge(T.sem["rq%d" % r], arr)
             V.tensor_copy(out, win).then_inc(gs[r], 1)
-    for part in (p["resp"][me][0:4], p["resp"][me][4:8]):
+    for part in p["respc"][me]:
         items = []
         for r in part:
             g.wait_ge(gs[r], 1)
@@ -250,7 +285,8 @@ def rank_program(g, core, T, topo):
                 items.append((cores[r], src, T.land[:, CAP * me:CAP * me + CAP], T.sem.resp))
         sent += fused(items)
 
-    total = sum(len(_bits(topo.mask(relay[(me, o)], core))) if (me, o) in relay else 2 for o in range(N) if o != me)
+    total = sum(len(_bits(topo.mask(relay[(me, o)], core))) if (me, o) in relay else p["respe"][(me, o)]
+                for o in range(N) if o != me)
     V.wait_ge(eFin, 1)
     V.wait_ge(eself, 1)
     V.wait_ge(T.sem.resp, total)

@@ -39,7 +39,7 @@ SCRATCH = {
     "pf": ("psum", [128, 512], "float32"),
 }
 SEMAPHORES = (["e%d" % i for i in range(NE)] + ["rq%d" % i for i in range(N)]
-              + ["resp", "sent", "rreq", "rresp", "idxl", "tabl", "st0", "st1"])
+              + ["resp", "sent", "rreq", "rresp", "idxl", "tabl", "st0", "entl", "finl"])
 
 _CACHE = {}
 
@@ -119,8 +119,19 @@ def _plan(T, topo):
             e = per(cores[o], [relay.get((r, o), cores[r]) for r in call])
             for r in call:
                 respe[(r, o)] = e
+    helper = [[x for x in world if x not in cores and topo.host(x) == topo.host(c) and topo.chip(x) == topo.chip(c)
+               and topo.die(x) == topo.die(c)][0] for c in cores]
+    entm = []
+    for r in range(n):
+        m = topo.mask(cores[r], helper[r])
+        for o in range(n):
+            if o != r:
+                m &= topo.mask(cores[r], relay.get((r, o), cores[o]))
+        entm.append(m)
     p = {"cores": cores, "relay": relay, "reqc": reqc, "respc": respc, "reqe": reqe, "respe": respe,
-         "by_relay": dict((v, k) for k, v in relay.items())}
+         "by_relay": dict((v, k) for k, v in relay.items()), "helper": helper,
+         "by_helper": dict((h, r) for r, h in enumerate(helper)), "entm": entm,
+         "ente": [len(_bits(m)) for m in entm]}
     _CACHE["p"] = p
     return p
 
@@ -138,6 +149,87 @@ def _relay_program(g, core, T, topo, p, r, o):
     g.wait_ge(T.sem.sent, len(_bits(m)) + len(_bits(m2)))
 
 
+def _slots(g, T, ev, sem_in, n_in, helper):
+    V, PE = g.vector, g.tensor
+    A = AluOpType
+    e_ones, e_hz, e_oval, e_tri, e_mk, e_c, e1, e3, eP, eZ, eS, e5 = [ev() for _ in range(12)]
+    eH = [ev() for _ in range(8)]
+    V.memset(T.onesb[:, 0:(1024 if helper else 128)], 1.0).then_inc(e_ones, 1)
+    V.memset(T.hpad[:, 0:64], 0.0).then_inc(e_hz, 1)
+    g.iota(T.oval[:, :], [[0, 8], [1, 9]], 0, 0, allow_small_or_imprecise_dtypes=True).then_inc(e_oval, 1)
+    g.wait_ge(e_ones, 1)
+    g.affine_select(T.tri[:, :], T.onesb[:, 0:128], [[1, 128]], A.is_gt, 0.0, 0, -1).then_inc(e_tri, 1)
+    V.wait_ge(e_oval, 1)
+    V.tensor_scalar(T.mk[:, :], T.oval[:, :], 1.0, None, A.min).then_inc(e_mk, 1)
+    V.tensor_scalar(T.c256[:, :], T.oval[:, :], 256.0, None, A.mult).then_inc(e_c, 1)
+    V.wait_ge(sem_in, n_in)
+    V.tensor_scalar(T.own_i[:, :], T.ent[:, :], 12, None, A.logical_shift_right).then_inc(e1, 1)
+    V.wait_ge(e1, 1)
+    V.tensor_copy(T.own_f[:, :], T.own_i[:, :]).then_inc(e3, 1)
+    V.wait_ge(e3, 1)
+    for b in range(8):
+        V.tensor_scalar(T.hpad[:, 64 + 9 * b:73 + 9 * b], T.oval[:, 0:9], T.own_f[:, b:b + 1], None,
+                        A.is_equal).then_inc(eH[b], 1)
+    PE.wait_ge(e_ones, 1)
+    PE.wait_ge(e_c, 1)
+    PE.matmul(T.pp[:, 0:72], T.onesb[0:1, 0:128], T.c256[0:1, :], True, False).then_inc(eP, 1)
+    PE.wait_ge(e_hz, 1)
+    for k in range(7, 0, -1):
+        PE.wait_ge(eH[7 - k], 1)
+        PE.matmul(T.pp[:, 0:72], T.onesb[:, 0:128], T.hpad[:, 64 - 9 * k:136 - 9 * k], False, False).then_inc(eP, 1)
+    PE.wait_ge(eH[7], 1)
+    PE.wait_ge(e_tri, 1)
+    PE.matmul(T.pp[:, 0:72], T.tri[:, :], T.hpad[:, 64:136], False, True).then_inc(eP, 1)
+    if not helper:
+        e2, e4 = ev(), ev()
+        V.tensor_scalar(T.loc_i[:, :], T.ent[:, :], R - 1, None, A.bitwise_and).then_inc(e2, 1)
+        V.wait_ge(e2, 1)
+        V.tensor_scalar(T.locm[:, :], T.loc_i[:, :], -2048.0, None, A.add).then_inc(e4, 1)
+        V.wait_ge(e4, 1)
+    V.wait_ge(eP, 9)
+    for b in range(8):
+        V.wait_ge(eH[b], 1)
+    V.tensor_tensor(T.zz[:, :], T.pp[:, 0:72], T.hpad[:, 64:136], A.mult).then_inc(eZ, 1)
+    V.wait_ge(eZ, 1)
+    V.wait_ge(e_mk, 1)
+    V.tensor_tensor_scan(T.sc[:, :], T.mk[:, :], T.zz[:, :], 0.0, A.mult, A.add).then_inc(eS, 1)
+    V.wait_ge(eS, 1)
+    V.tensor_copy(T.slot_i[:, :], T.sc[:, 8:72:9]).then_inc(e5, 1)
+    return e5
+
+
+def _helper_program(g, core, T, topo, p, r):
+    V, PE = g.vector, g.tensor
+    A = AluOpType
+    cnt = [0]
+
+    def ev():
+        cnt[0] += 1
+        return T.sem["e%d" % (cnt[0] - 1)]
+
+    e5 = _slots(g, T, ev, T.sem.entl, p["ente"][r], True)
+    e_sel, e6, e8, eF, eFin = [ev() for _ in range(5)]
+    g.affine_select(T.sel[:, :], T.onesb[:, :], [[-1, 8], [0, 8], [-8, 16]], A.is_equal, 0.0, 0, 1).then_inc(e_sel, 1)
+    V.wait_ge(e5, 1)
+    V.tensor_scalar(T.hl_i[:, 8:16], T.slot_i[:, :], 15, None, A.bitwise_and).then_inc(e6, 1)
+    V.tensor_scalar(T.hl_i[:, 16:24], T.slot_i[:, :], 4080, None, A.bitwise_and).then_inc(e6, 1)
+    V.wait_ge(e6, 2)
+    V.tensor_copy(T.hlb[:, :], T.hl_i[:, 8:24]).then_inc(e8, 1)
+    PE.wait_ge(e8, 1)
+    PE.wait_ge(e_sel, 1)
+    for h in range(8):
+        PE.matmul(T.pf[:, 8 * h:8 * h + 8], T.sel[:, 128 * h:128 * h + 128], T.hlb[:, 0:8], True, False).then_inc(eF, 1)
+        PE.matmul(T.pf[:, 8 * h:8 * h + 8], T.sel[:, 128 * h:128 * h + 128], T.hlb[:, 8:16], False, True).then_inc(eF, 1)
+    V.wait_ge(eF, 16)
+    V.tensor_copy(T.fin[:, :], T.pf[:, 0:64]).then_inc(eFin, 1)
+    cr = p["cores"][r]
+    m = topo.mask(core, cr)
+    rid, pid = topo.addr(cr, core)
+    g.wait_ge(eFin, 1)
+    g.remote_dma(T.fin[:, :], T.fin[:, :], T.sem.finl, T.sem.sent, pid, rid, m)
+    g.wait_ge(T.sem.sent, len(_bits(m)))
+
+
 def rank_program(g, core, T, topo):
     p = _plan(T, topo)
     me = T.rank_of(core)
@@ -145,6 +237,8 @@ def rank_program(g, core, T, topo):
         if core in p["by_relay"]:
             r, o = p["by_relay"][core]
             _relay_program(g, core, T, topo, p, r, o)
+        elif core in p["by_helper"]:
+            _helper_program(g, core, T, topo, p, p["by_helper"][core])
         return
     cores, relay = p["cores"], p["relay"]
     V, PE, S, SY = g.vector, g.tensor, g.scalar, g.sync
@@ -158,55 +252,20 @@ def rank_program(g, core, T, topo):
     SY.dma_start(T.ent[:, :], T.idx[:, :]).then_inc(T.sem.idxl, 16)
     SY.dma_start(T.tabs[:, :], T.tab[:, :]).then_inc(T.sem.tabl, 16)
 
-    e_ones, e_hz, e_oval, e_tri, e_i16, e_i144, e_sel, e_mk, e_c = [ev() for _ in range(9)]
-    V.memset(T.onesb[:, :], 1.0).then_inc(e_ones, 1)
-    V.memset(T.hpad[:, 0:64], 0.0).then_inc(e_hz, 1)
-    g.iota(T.oval[:, :], [[0, 8], [1, 9]], 0, 0, allow_small_or_imprecise_dtypes=True).then_inc(e_oval, 1)
-    g.wait_ge(e_ones, 1)
-    g.affine_select(T.tri[:, :], T.onesb[:, 0:128], [[1, 128]], A.is_gt, 0.0, 0, -1).then_inc(e_tri, 1)
+    e5 = _slots(g, T, ev, T.sem.idxl, 16, False)
+    e_i16, e_i144, e6, e7, eR, eO, eself, ey0, ey1 = [ev() for _ in range(9)]
     g.iota(T.i16[:, :], [[0, 8], [1, 16]], 0, 0, allow_small_or_imprecise_dtypes=True).then_inc(e_i16, 1)
     g.iota(T.i144[:, :], [[1, 144]], 0, 0, allow_small_or_imprecise_dtypes=True).then_inc(e_i144, 1)
-    g.affine_select(T.sel[:, :], T.onesb[:, :], [[-1, 8], [0, 8], [-8, 16]], A.is_equal, 0.0, 0, 1).then_inc(e_sel, 1)
-    V.wait_ge(e_oval, 1)
-    V.tensor_scalar(T.mk[:, :], T.oval[:, :], 1.0, None, A.min).then_inc(e_mk, 1)
-    V.tensor_scalar(T.c256[:, :], T.oval[:, :], 256.0, None, A.mult).then_inc(e_c, 1)
-
-    e1, e2, e3, e4, eH, eP, eZ, eS, e5, e6, e7, e8, eR, eO, eF, eFin, eself, ey0, ey1 = [ev() for _ in range(19)]
-    V.wait_ge(T.sem.idxl, 16)
-    V.tensor_scalar(T.own_i[:, :], T.ent[:, :], 12, None, A.logical_shift_right).then_inc(e1, 1)
-    V.wait_ge(e1, 1)
-    V.tensor_copy(T.own_f[:, :], T.own_i[:, :]).then_inc(e3, 1)
-    V.wait_ge(e3, 1)
-    for b in range(8):
-        V.tensor_scalar(T.hpad[:, 64 + 9 * b:73 + 9 * b], T.oval[:, 0:9], T.own_f[:, b:b + 1], None,
-                        A.is_equal).then_inc(eH, 1)
-    V.tensor_scalar(T.loc_i[:, :], T.ent[:, :], R - 1, None, A.bitwise_and).then_inc(e2, 1)
-    V.wait_ge(e2, 1)
-    V.tensor_scalar(T.locm[:, :], T.loc_i[:, :], -2048.0, None, A.add).then_inc(e4, 1)
-
-    for s, v in ((eH, 8), (e_hz, 1), (e_tri, 1), (e_ones, 1), (e_c, 1)):
-        PE.wait_ge(s, v)
-    PE.matmul(T.pp[:, 0:72], T.tri[:, :], T.hpad[:, 64:136], True, False).then_inc(eP, 1)
-    for k in range(1, 8):
-        PE.matmul(T.pp[:, 0:72], T.onesb[:, 0:128], T.hpad[:, 64 - 9 * k:136 - 9 * k], False, False).then_inc(eP, 1)
-    PE.matmul(T.pp[:, 0:72], T.onesb[0:1, 0:128], T.c256[0:1, :], False, True).then_inc(eP, 1)
-
-    V.wait_ge(eP, 9)
-    V.wait_ge(eH, 8)
-    V.tensor_tensor(T.zz[:, :], T.pp[:, 0:72], T.hpad[:, 64:136], A.mult).then_inc(eZ, 1)
-    V.wait_ge(eZ, 1)
-    V.wait_ge(e_mk, 1)
-    V.tensor_tensor_scan(T.sc[:, :], T.mk[:, :], T.zz[:, :], 0.0, A.mult, A.add).then_inc(eS, 1)
-    V.wait_ge(eS, 1)
-    V.tensor_copy(T.slot_i[:, :], T.sc[:, 8:72:9]).then_inc(e5, 1)
+    hc = p["helper"][me]
+    rid, pid = topo.addr(hc, core)
+    g.wait_ge(T.sem.idxl, 16)
+    g.remote_dma(T.ent[:, :], T.ent[:, :], T.sem.entl, T.sem.sent, pid, rid, p["entm"][me])
     V.wait_ge(e5, 1)
     V.tensor_scalar(T.hl_i[:, 0:8], T.slot_i[:, :], 4, None, A.logical_shift_right).then_inc(e6, 1)
     V.tensor_scalar(T.hl_i[:, 8:16], T.slot_i[:, :], 15, None, A.bitwise_and).then_inc(e6, 1)
-    V.tensor_scalar(T.hl_i[:, 16:24], T.slot_i[:, :], 4080, None, A.bitwise_and).then_inc(e6, 1)
-    V.wait_ge(e6, 3)
+    V.wait_ge(e6, 2)
     V.tensor_copy(T.hl_f[:, :], T.hl_i[:, 0:16]).then_inc(e7, 1)
     V.wait_ge(e7, 1)
-    V.wait_ge(e4, 1)
     V.wait_ge(e_i16, 1)
     V.wait_ge(e_i144, 1)
 
@@ -234,7 +293,7 @@ def rank_program(g, core, T, topo):
         g.remote_dma_fused(tr, local_sem=T.sem.sent)
         return per * len(items)
 
-    sent = 0
+    sent = p["ente"][me]
     g.wait_ge(eO, 1)
     for part in p["reqc"][me]:
         items = []
@@ -245,15 +304,6 @@ def rank_program(g, core, T, topo):
             else:
                 items.append((cores[o], src, T.rq[:, 16 * me:16 * me + 16], T.sem["rq%d" % me]))
         sent += fused(items)
-
-    V.tensor_copy(T.hlb[:, :], T.hl_i[:, 8:24]).then_inc(e8, 1)
-    PE.wait_ge(e8, 1)
-    PE.wait_ge(e_sel, 1)
-    for h in range(8):
-        PE.matmul(T.pf[:, 8 * h:8 * h + 8], T.sel[:, 128 * h:128 * h + 128], T.hlb[:, 0:8], True, False).then_inc(eF, 1)
-        PE.matmul(T.pf[:, 8 * h:8 * h + 8], T.sel[:, 128 * h:128 * h + 128], T.hlb[:, 8:16], False, True).then_inc(eF, 1)
-    V.wait_ge(eF, 16)
-    V.tensor_copy(T.fin[:, :], T.pf[:, 0:64]).then_inc(eFin, 1)
 
     S.wait_ge(eO, 1)
     S.wait_ge(T.sem.tabl, 16)
@@ -287,19 +337,18 @@ def rank_program(g, core, T, topo):
 
     total = sum(len(_bits(topo.mask(relay[(me, o)], core))) if (me, o) in relay else p["respe"][(me, o)]
                 for o in range(N) if o != me)
-    V.wait_ge(eFin, 1)
+    nfin = len(_bits(topo.mask(hc, core)))
+    V.wait_ge(T.sem.finl, nfin)
     V.wait_ge(eself, 1)
     V.wait_ge(T.sem.resp, total)
     V.tensor_copy(T.ybuf[:, 0:512], T.land[:, 0:N * CAP].indirect(T.fin[:, 0:32])).then_inc(ey0, 1)
-    S.wait_ge(eFin, 1)
+    S.wait_ge(T.sem.finl, nfin)
     S.wait_ge(eself, 1)
     S.wait_ge(T.sem.resp, total)
     S.activation(T.ybuf[:, 512:1024], T.land[:, 0:N * CAP].indirect(T.fin[:, 32:64]),
                  ActivationFunctionType.Copy).then_inc(ey1, 1)
     SY.wait_ge(ey0, 1)
-    SY.dma_start(T.y[:, 0:512], T.ybuf[:, 0:512]).then_inc(T.sem.st0, 16)
-    S.wait_ge(ey1, 1)
-    S.dma_start(T.y[:, 512:1024], T.ybuf[:, 512:1024]).then_inc(T.sem.st1, 16)
+    SY.wait_ge(ey1, 1)
+    SY.dma_start(T.y[:, :], T.ybuf[:, :]).then_inc(T.sem.st0, 16)
     SY.wait_ge(T.sem.st0, 16)
-    S.wait_ge(T.sem.st1, 16)
     g.wait_ge(T.sem.sent, sent)

@@ -55,32 +55,33 @@ def _plan(T, topo):
     n = len(cores)
     world = range(4 * topo.CORES_PER_HOST)
     rank_hosts = set(topo.host(c) for c in cores)
-    relay = {}
-    for r in range(n):
-        for o in range(n):
-            cr, co = cores[r], cores[o]
-            if r == o or topo.may_write(cr, co):
-                continue
-            far = near = None
-            chipc = []
-            for h in range(4):
-                if h in rank_hosts:
-                    continue
-                far, near = (cr, co) if topo.rack(topo.host(cr)) != topo.rack(h) else (co, cr)
-                chipc = [x for x in world if topo.host(x) == h and topo.chip(x) == topo.chip(far)]
-                if all(topo.may_write(cr, x) and topo.may_write(x, co) and topo.may_write(co, x)
-                       and topo.may_write(x, cr) for x in chipc):
-                    break
-            other = [x for x in chipc if topo.die(x) != topo.die(far)]
-            same = [x for x in chipc if topo.die(x) == topo.die(far)]
-            k = [c for c in cores if topo.host(c) == topo.host(near)].index(near)
-            if far == cr:
-                relay[(r, o)] = [same[0], same[2], other[3]][k]
-            else:
-                relay[(r, o)] = other[k]
 
     def hidx(a):
         return [c for c in cores if topo.host(c) == topo.host(cores[a])].index(cores[a])
+
+    helper = [[x for x in world if x not in cores and topo.host(x) == topo.host(c) and topo.chip(x) == topo.chip(c)
+               and topo.die(x) == topo.die(c)][0] for c in cores]
+    taken = set(cores) | set(helper)
+
+    def idle(h, like):
+        cc = [x for x in world if topo.host(x) == h and topo.chip(x) == topo.chip(like) and x not in taken]
+        return [x for x in cc if topo.die(x) == topo.die(like)], [x for x in cc if topo.die(x) != topo.die(like)]
+
+    far = [(r, o) for r in range(n) for o in range(n) if r != o and not topo.may_write(cores[r], cores[o])]
+    relay = {}
+    for r, o in far:
+        cr, co = cores[r], cores[o]
+        hs = [h for h in range(4) if h != topo.host(cr) and h != topo.host(co)]
+        ho = [h for h in hs if topo.rack(h) == topo.rack(topo.host(co))][0]
+        hr = [h for h in hs if topo.rack(h) == topo.rack(topo.host(cr))][0]
+        own_cable = ho in rank_hosts
+        if own_cable and hidx(r) == hidx(o):
+            relay[(r, o)] = idle(hr, co)[1][hidx(r)]
+        else:
+            same, other = idle(ho, cr)
+            picks = same[0::2] + other[::-1][0::2]
+            users = [x for (q, x) in far if q == r and not (own_cable and hidx(q) == hidx(x))]
+            relay[(r, o)] = picks[users.index(o)]
 
     def outer(a):
         return any((a, x) in relay for x in range(n))
@@ -109,27 +110,50 @@ def _plan(T, topo):
             e = per(cores[r], [relay.get((r, o), cores[o]) for o in call])
             for o in call:
                 reqe[(r, o)], when[(r, o)] = e, t
+    taken2 = taken | set(relay.values())
+    fwd = {}
+    for o in range(n):
+        co = cores[o]
+        cc = [x for x in world if topo.host(x) == topo.host(co) and topo.chip(x) == topo.chip(co) and x not in taken2]
+        seats = [helper[o], [x for x in cc if topo.die(x) == topo.die(co)][-1],
+                 [x for x in cc if topo.die(x) != topo.die(co)][0]]
+        for r in range(n):
+            if r != o and (r, o) not in relay and topo.rack(topo.host(cores[r])) != topo.rack(topo.host(co)):
+                fwd[(r, o)] = seats[(hidx(r) - hidx(o)) % len(seats)]
+
+    def engines(o, call):
+        if (call[0], o) in fwd:
+            out = _bits(topo.mask(cores[o], cores[call[0]]))
+            return [e for e in _bits(topo.mask(cores[o], fwd[(call[0], o)])) if e not in out]
+        return [e for e in range(16) if all((topo.mask(cores[o], relay.get((r, o), cores[r])) >> e) & 1 for r in call)]
+
     respc, respe = [], {}
     for o in range(n):
         late = sorted([r for r in range(n) if (r, o) in relay], key=lambda r: when[(r, o)])
         d = sorted([r for r in range(n) if r != o and (r, o) not in relay], key=lambda r: (when[(r, o)], (r - o) % n))
-        calls = [[r] for r in late] + ([[d[0]], d[1:]] if late else [d[0:len(d) // 2], d[len(d) // 2:]])
+        cross = [r for r in d if (r, o) in fwd]
+        plain = [r for r in d if (r, o) not in fwd]
+        fc = [cross[0:1], cross[1:]] if cross else []
+        if late:
+            calls = fc + [[r] for r in late] + ([plain] if cross else [[plain[0]], plain[1:]])
+        else:
+            calls = [plain[0:3]] + fc + [plain[3:]]
         respc.append(calls)
         for call in calls:
-            e = per(cores[o], [relay.get((r, o), cores[r]) for r in call])
+            e = len(engines(o, call)) // len(call)
             for r in call:
                 respe[(r, o)] = e
-    helper = [[x for x in world if x not in cores and topo.host(x) == topo.host(c) and topo.chip(x) == topo.chip(c)
-               and topo.die(x) == topo.die(c)][0] for c in cores]
     entm = []
     for r in range(n):
         m = topo.mask(cores[r], helper[r])
-        for o in range(n):
-            if o != r:
-                m &= topo.mask(cores[r], relay.get((r, o), cores[o]))
+        if not any(x == r for (_, x) in fwd):
+            for o in range(n):
+                if o != r:
+                    m &= topo.mask(cores[r], relay.get((r, o), cores[o]))
         entm.append(m)
     p = {"cores": cores, "relay": relay, "reqc": reqc, "respc": respc, "reqe": reqe, "respe": respe,
-         "by_relay": dict((v, k) for k, v in relay.items()), "helper": helper,
+         "by_relay": dict((v, k) for k, v in relay.items()), "helper": helper, "fwd": fwd, "engines": engines,
+         "by_fwd": dict((v, k) for k, v in fwd.items()),
          "by_helper": dict((h, r) for r, h in enumerate(helper)), "entm": entm,
          "ente": [len(_bits(m)) for m in entm]}
     _CACHE["p"] = p
@@ -142,11 +166,16 @@ def _relay_program(g, core, T, topo, p, r, o):
     rid, pid = topo.addr(co, core)
     g.wait_ge(T.sem.rreq, p["reqe"][(r, o)])
     g.remote_dma(T.rq[:, 16 * r:16 * r + 16], T.rq[:, 0:16], T.sem["rq%d" % r], T.sem.sent, pid, rid, m)
-    m2 = topo.mask(core, cr)
+    g.wait_ge(T.sem.sent, len(_bits(m)) + _forward(g, core, T, topo, p, r, o))
+
+
+def _forward(g, core, T, topo, p, r, o):
+    cr = p["cores"][r]
+    m = topo.mask(core, cr)
     rid, pid = topo.addr(cr, core)
     g.wait_ge(T.sem.rresp, p["respe"][(r, o)])
-    g.remote_dma(T.land[:, CAP * o:CAP * o + CAP], T.land[:, 0:CAP], T.sem.resp, T.sem.sent, pid, rid, m2)
-    g.wait_ge(T.sem.sent, len(_bits(m)) + len(_bits(m2)))
+    g.remote_dma(T.land[:, CAP * o:CAP * o + CAP], T.land[:, 0:CAP], T.sem.resp, T.sem.sent, pid, rid, m)
+    return len(_bits(m))
 
 
 def _slots(g, T, ev, sem_in, n_in, helper):
@@ -227,7 +256,11 @@ def _helper_program(g, core, T, topo, p, r):
     rid, pid = topo.addr(cr, core)
     g.wait_ge(eFin, 1)
     g.remote_dma(T.fin[:, :], T.fin[:, :], T.sem.finl, T.sem.sent, pid, rid, m)
-    g.wait_ge(T.sem.sent, len(_bits(m)))
+    sent = len(_bits(m))
+    if core in p["by_fwd"]:
+        q, o = p["by_fwd"][core]
+        sent += _forward(g, core, T, topo, p, q, o)
+    g.wait_ge(T.sem.sent, sent)
 
 
 def rank_program(g, core, T, topo):
@@ -239,8 +272,11 @@ def rank_program(g, core, T, topo):
             _relay_program(g, core, T, topo, p, r, o)
         elif core in p["by_helper"]:
             _helper_program(g, core, T, topo, p, p["by_helper"][core])
+        elif core in p["by_fwd"]:
+            r, o = p["by_fwd"][core]
+            g.wait_ge(T.sem.sent, _forward(g, core, T, topo, p, r, o))
         return
-    cores, relay = p["cores"], p["relay"]
+    cores, relay, fwd = p["cores"], p["relay"], p["fwd"]
     V, PE, S, SY = g.vector, g.tensor, g.scalar, g.sync
     A = AluOpType
     cnt = [0]
@@ -281,8 +317,7 @@ def rank_program(g, core, T, topo):
     V.wait_ge(eR, 8)
     V.tensor_scalar(T.offs[:, :], T.pr[:, 0:144], 2048.0, None, A.add).then_inc(eO, 1)
 
-    def fused(items):
-        eng = [i for i in range(16) if all((topo.mask(core, d) >> i) & 1 for d, _, _, _ in items)]
+    def fused(items, eng):
         per = len(eng) // len(items)
         tr = []
         for k, (d, src, dst, sem) in enumerate(items):
@@ -303,7 +338,7 @@ def rank_program(g, core, T, topo):
                 items.append((relay[(me, o)], src, T.rq[:, 0:16], T.sem.rreq))
             else:
                 items.append((cores[o], src, T.rq[:, 16 * me:16 * me + 16], T.sem["rq%d" % me]))
-        sent += fused(items)
+        sent += fused(items, [i for i in range(16) if all((topo.mask(core, d) >> i) & 1 for d, _, _, _ in items)])
 
     S.wait_ge(eO, 1)
     S.wait_ge(T.sem.tabl, 16)
@@ -331,12 +366,17 @@ def rank_program(g, core, T, topo):
             src = T.stage[:, CAP * r:CAP * r + CAP]
             if (r, me) in relay:
                 items.append((relay[(r, me)], src, T.land[:, 0:CAP], T.sem.rresp))
+            elif (r, me) in fwd:
+                items.append((fwd[(r, me)], src, T.land[:, 0:CAP], T.sem.rresp))
             else:
                 items.append((cores[r], src, T.land[:, CAP * me:CAP * me + CAP], T.sem.resp))
-        sent += fused(items)
+        sent += fused(items, p["engines"](me, part))
 
-    total = sum(len(_bits(topo.mask(relay[(me, o)], core))) if (me, o) in relay else p["respe"][(me, o)]
-                for o in range(N) if o != me)
+    total = 0
+    for o in range(N):
+        if o != me:
+            last = relay.get((me, o), fwd.get((me, o)))
+            total += p["respe"][(me, o)] if last is None else len(_bits(topo.mask(last, core)))
     nfin = len(_bits(topo.mask(hc, core)))
     V.wait_ge(T.sem.finl, nfin)
     V.wait_ge(eself, 1)

from concourse.bass import DstId, RemoteDMATransfer
from concourse.mybir import AluOpType, ActivationFunctionType

N, R, L, CAP = 9, 4096, 1024, 256
NE = 80

SCRATCH = {
    "tabs": ("sbuf", [128, R], "bfloat16"),
    "land": ("sbuf", [128, N * CAP], "bfloat16"),
    "stage": ("sbuf", [128, N * CAP], "bfloat16"),
    "ybuf": ("sbuf", [128, L], "bfloat16"),
    "ent": ("sbuf", [128, 8], "int32"),
    "own_i": ("sbuf", [128, 8], "int32"),
    "loc_i": ("sbuf", [128, 8], "int32"),
    "own_f": ("sbuf", [128, 8], "float32"),
    "locm": ("sbuf", [128, 8], "float32"),
    "oval": ("sbuf", [128, 72], "float32"),
    "mk": ("sbuf", [128, 72], "float32"),
    "c256": ("sbuf", [128, 72], "bfloat16"),
    "hpad": ("sbuf", [128, 136], "bfloat16"),
    "onesb": ("sbuf", [128, 1024], "bfloat16"),
    "tri": ("sbuf", [128, 128], "bfloat16"),
    "sel": ("sbuf", [128, 1024], "bfloat16"),
    "i16": ("sbuf", [128, 128], "bfloat16"),
    "i144": ("sbuf", [128, 144], "bfloat16"),
    "zz": ("sbuf", [128, 72], "float32"),
    "sc": ("sbuf", [128, 72], "float32"),
    "slot_i": ("sbuf", [128, 8], "int32"),
    "hl_i": ("sbuf", [128, 24], "int32"),
    "hl_f": ("sbuf", [128, 16], "float32"),
    "hlb": ("sbuf", [128, 16], "bfloat16"),
    "lt": ("sbuf", [128, 1024], "float16"),
    "rh": ("sbuf", [128, 1152], "float16"),
    "offs": ("sbuf", [128, 16 * N], "uint16"),
    "rq": ("sbuf", [128, 16 * N], "uint16"),
    "fin": ("sbuf", [128, 64], "uint16"),
    "pp": ("psum", [128, 512], "float32"),
    "pr": ("psum", [128, 512], "float32"),
    "pf": ("psum", [128, 512], "float32"),
}
SEMAPHORES = (["e%d" % i for i in range(NE)] + ["rq%d" % i for i in range(N)]
              + ["resp", "sent", "rreq", "rresp", "idxl", "tabl", "st0", "entl", "finl"])

_CACHE = {}


def _bits(m):
    return [i for i in range(16) if (m >> i) & 1]


def _plan(T, topo):
    if "p" in _CACHE:
        return _CACHE["p"]
    cores = list(T.cores)
    n = len(cores)
    world = range(4 * topo.CORES_PER_HOST)
    rank_hosts = set(topo.host(c) for c in cores)

    def hidx(a):
        return [c for c in cores if topo.host(c) == topo.host(cores[a])].index(cores[a])

    helper = [[x for x in world if x not in cores and topo.host(x) == topo.host(c) and topo.chip(x) == topo.chip(c)
               and topo.die(x) == topo.die(c)][0] for c in cores]
    taken = set(cores) | set(helper)

    def idle(h, like):
        cc = [x for x in world if topo.host(x) == h and topo.chip(x) == topo.chip(like) and x not in taken]
        return [x for x in cc if topo.die(x) == topo.die(like)], [x for x in cc if topo.die(x) != topo.die(like)]

    far = [(r, o) for r in range(n) for o in range(n) if r != o and not topo.may_write(cores[r], cores[o])]
    relay = {}
    for r, o in far:
        cr, co = cores[r], cores[o]
        hs = [h for h in range(4) if h != topo.host(cr) and h != topo.host(co)]
        ho = [h for h in hs if topo.rack(h) == topo.rack(topo.host(co))][0]
        hr = [h for h in hs if topo.rack(h) == topo.rack(topo.host(cr))][0]
        own_cable = ho in rank_hosts
        if own_cable and hidx(r) == hidx(o):
            relay[(r, o)] = idle(hr, co)[1][hidx(r)]
        else:
            same, other = idle(ho, cr)
            picks = same[0::2] + other[::-1][0::2]
            users = [x for (q, x) in far if q == r and not (own_cable and hidx(q) == hidx(x))]
            relay[(r, o)] = picks[users.index(o)]

    def outer(a):
        return any((a, x) in relay for x in range(n))

    reqc = []
    for r in range(n):
        k = hidx(r)
        rel = sorted([o for o in range(n) if (r, o) in relay], key=lambda o: (hidx(o) - k) % n)
        rest = [o for o in range(n) if o != r and (r, o) not in relay]
        if rel:
            mids = [o for o in rest if not outer(o)]
            d0 = mids[k % len(mids)]
            reqc.append([[o] for o in rel] + [[d0], [o for o in rest if o != d0]])
        else:
            early = [o for o in rest if topo.host(cores[o]) == topo.host(cores[r]) or hidx(o) == k]
            reqc.append([early, [o for o in rest if o not in early]])

    def per(src, dests):
        return min(len(_bits(topo.mask(src, d))) for d in dests) // len(dests)

    reqe, when = {}, {}
    for r in range(n):
        t = 0
        for call in reqc[r]:
            t += len(call)
            e = per(cores[r], [relay.get((r, o), cores[o]) for o in call])
            for o in call:
                reqe[(r, o)], when[(r, o)] = e, t
    taken2 = taken | set(relay.values())
    fwd = {}
    for o in range(n):
        co = cores[o]
        cc = [x for x in world if topo.host(x) == topo.host(co) and topo.chip(x) == topo.chip(co) and x not in taken2]
        seats = [helper[o], [x for x in cc if topo.die(x) == topo.die(co)][-1],
                 [x for x in cc if topo.die(x) != topo.die(co)][0]]
        for r in range(n):
            if r != o and (r, o) not in relay and topo.rack(topo.host(cores[r])) != topo.rack(topo.host(co)):
                fwd[(r, o)] = seats[(hidx(r) - hidx(o)) % len(seats)]

    def engines(o, call):
        if (call[0], o) in fwd:
            out = _bits(topo.mask(cores[o], cores[call[0]]))
            return [e for e in _bits(topo.mask(cores[o], fwd[(call[0], o)])) if e not in out]
        return [e for e in range(16) if all((topo.mask(cores[o], relay.get((r, o), cores[r])) >> e) & 1 for r in call)]

    respc, respe = [], {}
    for o in range(n):
        late = sorted([r for r in range(n) if (r, o) in relay], key=lambda r: when[(r, o)])
        d = sorted([r for r in range(n) if r != o and (r, o) not in relay], key=lambda r: (when[(r, o)], (r - o) % n))
        cross = [r for r in d if (r, o) in fwd]
        plain = [r for r in d if (r, o) not in fwd]
        fc = [cross[0:1], cross[1:]] if cross else []
        if late:
            calls = fc + [[r] for r in late] + ([plain] if cross else [[plain[0]], plain[1:]])
        else:
            calls = [plain[0:3]] + fc + [plain[3:]]
        respc.append(calls)
        for call in calls:
            e = len(engines(o, call)) // len(call)
            for r in call:
                respe[(r, o)] = e
    entm = []
    for r in range(n):
        m = topo.mask(cores[r], helper[r])
        if not any(x == r for (_, x) in fwd):
            for o in range(n):
                if o != r:
                    m &= topo.mask(cores[r], relay.get((r, o), cores[o]))
        entm.append(m)
    p = {"cores": cores, "relay": relay, "reqc": reqc, "respc": respc, "reqe": reqe, "respe": respe,
         "by_relay": dict((v, k) for k, v in relay.items()), "helper": helper, "fwd": fwd, "engines": engines,
         "by_fwd": dict((v, k) for k, v in fwd.items()),
         "by_helper": dict((h, r) for r, h in enumerate(helper)), "entm": entm,
         "ente": [len(_bits(m)) for m in entm]}
    _CACHE["p"] = p
    return p


def _relay_program(g, core, T, topo, p, r, o):
    cr, co = p["cores"][r], p["cores"][o]
    m = topo.mask(core, co)
    rid, pid = topo.addr(co, core)
    g.wait_ge(T.sem.rreq, p["reqe"][(r, o)])
    g.remote_dma(T.rq[:, 16 * r:16 * r + 16], T.rq[:, 0:16], T.sem["rq%d" % r], T.sem.sent, pid, rid, m)
    g.wait_ge(T.sem.sent, len(_bits(m)) + _forward(g, core, T, topo, p, r, o))


def _forward(g, core, T, topo, p, r, o):
    cr = p["cores"][r]
    m = topo.mask(core, cr)
    rid, pid = topo.addr(cr, core)
    g.wait_ge(T.sem.rresp, p["respe"][(r, o)])
    g.remote_dma(T.land[:, CAP * o:CAP * o + CAP], T.land[:, 0:CAP], T.sem.resp, T.sem.sent, pid, rid, m)
    return len(_bits(m))


def _slots(g, T, ev, sem_in, n_in, helper):
    V, PE = g.vector, g.tensor
    A = AluOpType
    e_ones, e_hz, e_oval, e_tri, e_mk, e_c, e1, e3, eP, eZ, eS, e5 = [ev() for _ in range(12)]
    eH = [ev() for _ in range(8)]
    V.memset(T.onesb[:, 0:(1024 if helper else 128)], 1.0).then_inc(e_ones, 1)
    V.memset(T.hpad[:, 0:64], 0.0).then_inc(e_hz, 1)
    g.iota(T.oval[:, :], [[0, 8], [1, 9]], 0, 0, allow_small_or_imprecise_dtypes=True).then_inc(e_oval, 1)
    g.wait_ge(e_ones, 1)
    g.affine_select(T.tri[:, :], T.onesb[:, 0:128], [[1, 128]], A.is_gt, 0.0, 0, -1).then_inc(e_tri, 1)
    V.wait_ge(e_oval, 1)
    V.tensor_scalar(T.mk[:, :], T.oval[:, :], 1.0, None, A.min).then_inc(e_mk, 1)
    V.tensor_scalar(T.c256[:, :], T.oval[:, :], 256.0, None, A.mult).then_inc(e_c, 1)
    V.wait_ge(sem_in, n_in)
    V.tensor_scalar(T.own_i[:, :], T.ent[:, :], 12, None, A.logical_shift_right).then_inc(e1, 1)
    V.wait_ge(e1, 1)
    V.tensor_copy(T.own_f[:, :], T.own_i[:, :]).then_inc(e3, 1)
    V.wait_ge(e3, 1)
    for b in range(8):
        V.tensor_scalar(T.hpad[:, 64 + 9 * b:73 + 9 * b], T.oval[:, 0:9], T.own_f[:, b:b + 1], None,
                        A.is_equal).then_inc(eH[b], 1)
    PE.wait_ge(e_ones, 1)
    PE.wait_ge(e_c, 1)
    PE.matmul(T.pp[:, 0:72], T.onesb[0:1, 0:128], T.c256[0:1, :], True, False).then_inc(eP, 1)
    PE.wait_ge(e_hz, 1)
    for k in range(7, 0, -1):
        PE.wait_ge(eH[7 - k], 1)
        PE.matmul(T.pp[:, 0:72], T.onesb[:, 0:128], T.hpad[:, 64 - 9 * k:136 - 9 * k], False, False).then_inc(eP, 1)
    PE.wait_ge(eH[7], 1)
    PE.wait_ge(e_tri, 1)
    PE.matmul(T.pp[:, 0:72], T.tri[:, :], T.hpad[:, 64:136], False, True).then_inc(eP, 1)
    if not helper:
        e2, e4 = ev(), ev()
        V.tensor_scalar(T.loc_i[:, :], T.ent[:, :], R - 1, None, A.bitwise_and).then_inc(e2, 1)
        V.wait_ge(e2, 1)
        V.tensor_scalar(T.locm[:, :], T.loc_i[:, :], -2048.0, None, A.add).then_inc(e4, 1)
        V.wait_ge(e4, 1)
    V.wait_ge(eP, 9)
    for b in range(8):
        V.wait_ge(eH[b], 1)
    V.tensor_tensor(T.zz[:, :], T.pp[:, 0:72], T.hpad[:, 64:136], A.mult).then_inc(eZ, 1)
    V.wait_ge(eZ, 1)
    V.wait_ge(e_mk, 1)
    V.tensor_tensor_scan(T.sc[:, :], T.mk[:, :], T.zz[:, :], 0.0, A.mult, A.add).then_inc(eS, 1)
    V.wait_ge(eS, 1)
    V.tensor_copy(T.slot_i[:, :], T.sc[:, 8:72:9]).then_inc(e5, 1)
    return e5


def _helper_program(g, core, T, topo, p, r):
    V, PE = g.vector, g.tensor
    A = AluOpType
    cnt = [0]

    def ev():
        cnt[0] += 1
        return T.sem["e%d" % (cnt[0] - 1)]

    e5 = _slots(g, T, ev, T.sem.entl, p["ente"][r], True)
    e_sel, e6, e8, eF, eFin = [ev() for _ in range(5)]
    g.affine_select(T.sel[:, :], T.onesb[:, :], [[-1, 8], [0, 8], [-8, 16]], A.is_equal, 0.0, 0, 1).then_inc(e_sel, 1)
    V.wait_ge(e5, 1)
    V.tensor_scalar(T.hl_i[:, 8:16], T.slot_i[:, :], 15, None, A.bitwise_and).then_inc(e6, 1)
    V.tensor_scalar(T.hl_i[:, 16:24], T.slot_i[:, :], 4080, None, A.bitwise_and).then_inc(e6, 1)
    V.wait_ge(e6, 2)
    V.tensor_copy(T.hlb[:, :], T.hl_i[:, 8:24]).then_inc(e8, 1)
    PE.wait_ge(e8, 1)
    PE.wait_ge(e_sel, 1)
    for h in range(8):
        PE.matmul(T.pf[:, 8 * h:8 * h + 8], T.sel[:, 128 * h:128 * h + 128], T.hlb[:, 0:8], True, False).then_inc(eF, 1)
        PE.matmul(T.pf[:, 8 * h:8 * h + 8], T.sel[:, 128 * h:128 * h + 128], T.hlb[:, 8:16], False, True).then_inc(eF, 1)
    V.wait_ge(eF, 16)
    V.tensor_copy(T.fin[:, :], T.pf[:, 0:64]).then_inc(eFin, 1)
    cr = p["cores"][r]
    m = topo.mask(core, cr)
    rid, pid = topo.addr(cr, core)
    g.wait_ge(eFin, 1)
    g.remote_dma(T.fin[:, :], T.fin[:, :], T.sem.finl, T.sem.sent, pid, rid, m)
    sent = len(_bits(m))
    if core in p["by_fwd"]:
        q, o = p["by_fwd"][core]
        sent += _forward(g, core, T, topo, p, q, o)
    g.wait_ge(T.sem.sent, sent)


def rank_program(g, core, T, topo):
    p = _plan(T, topo)
    me = T.rank_of(core)
    if me is None:
        if core in p["by_relay"]:
            r, o = p["by_relay"][core]
            _relay_program(g, core, T, topo, p, r, o)
        elif core in p["by_helper"]:
            _helper_program(g, core, T, topo, p, p["by_helper"][core])
        elif core in p["by_fwd"]:
            r, o = p["by_fwd"][core]
            g.wait_ge(T.sem.sent, _forward(g, core, T, topo, p, r, o))
        return
    cores, relay, fwd = p["cores"], p["relay"], p["fwd"]
    V, PE, S, SY = g.vector, g.tensor, g.scalar, g.sync
    A = AluOpType
    cnt = [0]

    def ev():
        cnt[0] += 1
        return T.sem["e%d" % (cnt[0] - 1)]

    SY.dma_start(T.ent[:, :], T.idx[:, :]).then_inc(T.sem.idxl, 16)
    SY.dma_start(T.tabs[:, :], T.tab[:, :]).then_inc(T.sem.tabl, 16)

    e5 = _slots(g, T, ev, T.sem.idxl, 16, False)
    e_i16, e_i144, e6, e7, eR, eO, eself, ey0, ey1 = [ev() for _ in range(9)]
    g.iota(T.i16[:, :], [[0, 8], [1, 16]], 0, 0, allow_small_or_imprecise_dtypes=True).then_inc(e_i16, 1)
    g.iota(T.i144[:, :], [[1, 144]], 0, 0, allow_small_or_imprecise_dtypes=True).then_inc(e_i144, 1)
    hc = p["helper"][me]
    rid, pid = topo.addr(hc, core)
    g.wait_ge(T.sem.idxl, 16)
    g.remote_dma(T.ent[:, :], T.ent[:, :], T.sem.entl, T.sem.sent, pid, rid, p["entm"][me])
    V.wait_ge(e5, 1)
    V.tensor_scalar(T.hl_i[:, 0:8], T.slot_i[:, :], 4, None, A.logical_shift_right).then_inc(e6, 1)
    V.tensor_scalar(T.hl_i[:, 8:16], T.slot_i[:, :], 15, None, A.bitwise_and).then_inc(e6, 1)
    V.wait_ge(e6, 2)
    V.tensor_copy(T.hl_f[:, :], T.hl_i[:, 0:16]).then_inc(e7, 1)
    V.wait_ge(e7, 1)
    V.wait_ge(e_i16, 1)
    V.wait_ge(e_i144, 1)

    for b in range(8):
        eb = ev()
        V.tensor_scalar(T.lt[:, 128 * b:128 * b + 128], T.i16[:, :], T.hl_f[:, 8 + b:9 + b], None,
                        A.is_equal).then_inc(eb, 1)
        V.tensor_scalar(T.rh[:, 144 * b:144 * b + 144], T.i144[:, :], T.hl_f[:, b:b + 1], T.locm[:, b:b + 1],
                        A.is_equal, A.mult).then_inc(eb, 1)
        PE.wait_ge(eb, 2)
        PE.matmul(T.pr[:, 0:144], T.lt[:, 128 * b:128 * b + 128], T.rh[:, 144 * b:144 * b + 144],
                  b == 0, b == 7).then_inc(eR, 1)
    V.wait_ge(eR, 8)
    V.tensor_scalar(T.offs[:, :], T.pr[:, 0:144], 2048.0, None, A.add).then_inc(eO, 1)

    def fused(items, eng):
        per = len(eng) // len(items)
        tr = []
        for k, (d, src, dst, sem) in enumerate(items):
            rid, pid = topo.addr(d, core)
            tr.append(RemoteDMATransfer(dst_ids=[DstId(rid=rid, pnc=pid)],
                                        dma_engine_mask=sum(1 << e for e in eng[per * k:per * k + per]),
                                        remote_sem=sem, src=src, dst=dst))
        g.remote_dma_fused(tr, local_sem=T.sem.sent)
        return per * len(items)

    sent = p["ente"][me]
    g.wait_ge(eO, 1)
    for part in p["reqc"][me]:
        items = []
        for o in part:
            src = T.offs[:, 16 * o:16 * o + 16]
            if (me, o) in relay:
                items.append((relay[(me, o)], src, T.rq[:, 0:16], T.sem.rreq))
            else:
                items.append((cores[o], src, T.rq[:, 16 * me:16 * me + 16], T.sem["rq%d" % me]))
        sent += fused(items, [i for i in range(16) if all((topo.mask(core, d) >> i) & 1 for d, _, _, _ in items)])

    S.wait_ge(eO, 1)
    S.wait_ge(T.sem.tabl, 16)
    V.wait_ge(T.sem.tabl, 16)
    S.activation(T.land[:, CAP * me:CAP * me + CAP], T.tabs[:, 0:R].indirect(T.offs[:, 16 * me:16 * me + 16]),
                 ActivationFunctionType.Copy).then_inc(eself, 1)
    gs = {}
    order = [r for call in p["respc"][me] for r in call]
    has_late = any((r, me) in relay for r in order)
    for k, r in enumerate(order):
        gs[r] = ev()
        arr = len(_bits(topo.mask(relay[(r, me)], core))) if (r, me) in relay else p["reqe"][(r, me)]
        win = T.tabs[:, 0:R].indirect(T.rq[:, 16 * r:16 * r + 16])
        out = T.stage[:, CAP * r:CAP * r + CAP]
        if ((r, me) in relay) if has_late else (k % 2 == 0):
            S.wait_ge(T.sem["rq%d" % r], arr)
            S.activation(out, win, ActivationFunctionType.Copy).then_inc(gs[r], 1)
        else:
            V.wait_ge(T.sem["rq%d" % r], arr)
            V.tensor_copy(out, win).then_inc(gs[r], 1)
    for part in p["respc"][me]:
        items = []
        for r in part:
            g.wait_ge(gs[r], 1)
            src = T.stage[:, CAP * r:CAP * r + CAP]
            if (r, me) in relay:
                items.append((relay[(r, me)], src, T.land[:, 0:CAP], T.sem.rresp))
            elif (r, me) in fwd:
                items.append((fwd[(r, me)], src, T.land[:, 0:CAP], T.sem.rresp))
            else:
                items.append((cores[r], src, T.land[:, CAP * me:CAP * me + CAP], T.sem.resp))
        sent += fused(items, p["engines"](me, part))

    total = 0
    for o in range(N):
        if o != me:
            last = relay.get((me, o), fwd.get((me, o)))
            total += p["respe"][(me, o)] if last is None else len(_bits(topo.mask(last, core)))
    nfin = len(_bits(topo.mask(hc, core)))
    V.wait_ge(T.sem.finl, nfin)
    V.wait_ge(eself, 1)
    V.wait_ge(T.sem.resp, total)
    V.tensor_copy(T.ybuf[:, 0:512], T.land[:, 0:N * CAP].indirect(T.fin[:, 0:32])).then_inc(ey0, 1)
    S.wait_ge(T.sem.finl, nfin)
    S.wait_ge(eself, 1)
    S.wait_ge(T.sem.resp, total)
    S.activation(T.ybuf[:, 512:1024], T.land[:, 0:N * CAP].indirect(T.fin[:, 32:64]),
                 ActivationFunctionType.Copy).then_inc(ey1, 1)
    SY.wait_ge(ey0, 1)
    SY.wait_ge(ey1, 1)
    SY.dma_start(T.y[:, :], T.ybuf[:, :]).then_inc(T.sem.st0, 16)
    SY.wait_ge(T.sem.st0, 16)
    g.wait_ge(T.sem.sent, sent)
